import numpy as np
import ml_dtypes


def mxq(x, axis, fmt="e4m3"):
    dtype, down = {"e4m3": (ml_dtypes.float8_e4m3fn, 7), "e5m2": (ml_dtypes.float8_e5m2, 14)}[fmt]
    v = np.moveaxis(np.asarray(x, np.float32).astype(ml_dtypes.bfloat16).astype(np.float64), axis, -1)
    blocks = v.reshape(v.shape[:-1] + (-1, 32))
    amax = np.abs(blocks).max(-1, keepdims=True)
    byte = np.maximum(np.where(amax > 0, np.frexp(amax)[1] - 1 + 127, 0) - down, 1)
    scale = np.exp2(byte - 127.0)
    codes = (blocks / scale).astype(np.float32).astype(dtype).astype(np.float64)
    return np.moveaxis((codes * scale).reshape(v.shape), -1, axis)


WIDE = False


def mx_kscale(k):
    if not WIDE:
        return np.ones(k)
    levels = np.array([10, -10, 5, -5, 0])
    if k % 512:
        return np.exp2(np.random.permutation(np.resize(levels, k // 32))).repeat(32)
    a = np.empty((k // 512, 16))
    for p in range(k // 512):
        a[p, :8] = np.random.permutation(np.resize(levels, 8))
        for g in range(8):
            far = levels[np.abs(levels - a[p, g]) >= 10]
            a[p, g + 8] = far[np.random.randint(len(far))]
    return np.exp2(a.ravel()).repeat(32)


def f64(x):
    return np.asarray(x).astype(np.float64)


def striped(idx):
    return np.tile(np.asarray(idx).reshape(-1, 16).T, (8, 1)).astype(np.uint16)


def unstriped(offs):
    return offs[:16].T.reshape(-1).astype(np.int64)


E2M1 = np.array([0.0, 0.5, 1.0, 1.5, 2.0, 3.0, 4.0, 6.0, -0.0, -0.5, -1.0, -1.5, -2.0, -3.0, -4.0, -6.0])


def pack_weight(w, fmt):
    k, n = w.shape
    w = f64(np.asarray(w, np.float32).astype(ml_dtypes.bfloat16)).reshape(k // 32, 32, n)
    amax = np.abs(w).max(1)
    if fmt == "e4m3":
        byte = np.frexp(amax)[1] - 1 + 127 - 7
    else:
        mant, ex = np.frexp(amax / 6.0)
        byte = np.where(mant > 0.5, ex, ex - 1) + 127
    byte = np.clip(np.where(amax > 0, byte, 1), 1, 254)
    scaled = (w * np.exp2(127.0 - byte)[:, None, :]).reshape(k, n).astype(np.float32)
    by_word = np.ascontiguousarray(scaled.reshape(k // 512, 128, 4, n).transpose(0, 1, 3, 2))
    if fmt == "e4m3":
        words = by_word.astype(ml_dtypes.float8_e4m3fn).view(np.uint8)
    else:
        c = by_word.astype(ml_dtypes.float4_e2m1fn).view(np.uint8) & 0xF
        words = (c[..., 0::2] | (c[..., 1::2] << 4)).reshape(k // 512, 128, 2 * n)
    return np.ascontiguousarray(words), np.ascontiguousarray(byte.astype(np.uint8).reshape(k // 512, 16, n))


def unpack_weight(words, scales, fmt):
    g, _, n = scales.shape
    words = np.ascontiguousarray(words).reshape(g, 128, n, -1)
    if fmt == "e4m3":
        vals = words.view(ml_dtypes.float8_e4m3fn).astype(np.float64)
    else:
        nib = np.empty((g, 128, n, 4), np.uint8)
        nib[..., 0::2] = words & 0xF
        nib[..., 1::2] = words >> 4
        vals = E2M1[nib]
    vals = vals * np.repeat(np.exp2(scales.astype(np.float64) - 127.0), 8, axis=1)[..., None]
    return vals.transpose(0, 1, 3, 2).reshape(g * 512, n)


def sigmoid(v):
    return 1.0 / (1.0 + np.exp(-v))


B, N, T, D, NQ = 1, 512, 2048, 1024, 512
DV = 512


def sgn(shape):
    return np.random.uniform(0.5, 2.0, shape) * np.where(np.random.standard_normal(shape) < 0, -1.0, 1.0)


def setup_inputs():
    n = np.random.standard_normal
    idx = np.random.permutation(T)[:B * N]
    s = mx_kscale(D)[:, None]
    u = mx_kscale(N)
    ut = np.ones(T)
    ut[idx] = u
    kp = pack_weight(n((D, T)) / s, "e2m1")
    cp = pack_weight(n((D, T)) / s, "e2m1")
    return {
        "qT": (n((B, D, NQ)) * s * (1.00 / np.sqrt(D))).astype(np.float32),
        "k_words": np.ascontiguousarray(kp[0].reshape(1, 2, 128, T, 2).transpose(0, 2, 3, 1, 4)).reshape(1, 128, T, 4),
        "k_scales": kp[1],
        "c_words": np.ascontiguousarray(cp[0].reshape(1, 2, 128, T, 2).transpose(0, 2, 3, 1, 4)).reshape(1, 128, T, 4),
        "c_scales": cp[1],
        "vT": (n((DV, T)) / ut).astype(np.float32),
        "th": (n((B, 1, NQ)) + 1).astype(np.float32),
        "og": (n((B, NQ, DV))).astype(np.float32),
        "us": (sgn((B, N, 1)) * u[:, None]).astype(np.float32),
        "offs": striped(idx),
    }


def reference(qT, k_words, k_scales, c_words, c_scales, vT, th, og, us, offs):
    idx = unstriped(offs)
    pick = lambda x, which: x[:, which].reshape(x.shape[0], B, -1).transpose(1, 0, 2)
    k = unpack_weight(k_words.reshape(1, 128, T, 2, 2).transpose(0, 3, 1, 2, 4).reshape(2, 128, 2 * T), k_scales, "e2m1")
    kg = pick(k, idx)
    c = unpack_weight(c_words.reshape(1, 128, T, 2, 2).transpose(0, 3, 1, 2, 4).reshape(2, 128, 2 * T), c_scales, "e2m1")
    cg = pick(c, idx)
    qq = mxq(f64(qT), 1, "e4m3")
    a = kg.transpose(0, 2, 1) @ qq
    z = cg.transpose(0, 2, 1) @ qq
    y = sigmoid(np.maximum(a, z) - f64(th)) * f64(us)
    wq = mxq(y, 1, "e4m3")
    o = wq.transpose(0, 2, 1) @ mxq(pick(f64(vT), idx).transpose(0, 2, 1), 1, "e4m3")
    r_ = o * sigmoid(f64(og))
    return r_

@@ -1,0 +1,220 @@
+from contextlib import ExitStack
+
+import concourse.mybir as mybir
+from concourse.masks import make_identity
+
+F32 = mybir.dt.float32
+BF16 = mybir.dt.bfloat16
+I32 = mybir.dt.int32
+U32 = mybir.dt.uint32
+U16 = mybir.dt.uint16
+U8 = mybir.dt.uint8
+FP8X4 = mybir.dt.float8_e4m3fn_x4
+FP4X4 = mybir.dt.float4_e2m1fn_x4
+ACT = mybir.ActivationFunctionType
+ALU = mybir.AluOpType
+
+P = 128
+SLOTS = 512
+TOKENS = 2048
+D = 1024
+NQ = 512
+DV = 512
+PACK = 4
+PASSES = D // (P * PACK)
+Q_TILES = NQ // P
+E_BLOCKS = DV // P
+
+FLOPS = 2 * 2 * SLOTS * D * NQ + 2 * NQ * SLOTS * DV
+
+
+def tile_attend_at_proto_topk_kernel(tc, qT, k_words, k_scales, c_words, c_scales, vT, th, og, us, offs, out):
+    nc = tc.nc
+    with ExitStack() as ctx:
+        held = ctx.enter_context(tc.tile_pool(name="held", bufs=1))
+        work = ctx.enter_context(tc.tile_pool(name="work", bufs=2))
+        psum = ctx.enter_context(tc.psum_pool(name="psum", bufs=2))
+
+        offsets = held.tile([P, SLOTS // 16], U16, name="offsets")
+        nc.sync.dma_start(offsets[:], offs)
+
+        warm_in = held.tile([P, 8], F32, name="warm_in")
+        warm_out = held.tile([P, 8], F32, name="warm_out")
+        nc.vector.memset(warm_in[:], 0.0)
+        nc.scalar.activation(warm_out[:], warm_in[:], ACT.Sigmoid)
+
+        def load_scale_pool(name, scales, queue):
+            pool_tile = held.tile([P, TOKENS], U8, name=name, align_bytes=64)
+            nc.vector.memset(pool_tile[:].bitcast(I32), 0)
+            rows = scales.rearrange("o (q r) t -> r q o t", r=4)
+            for r in range(4):
+                queue.dma_start(pool_tile[r:P:16, :].bitcast(I32), rows[r].bitcast(I32))
+            return pool_tile
+
+        q_raw = []
+        for o in range(PASSES):
+            raw = held.tile([P, PACK, NQ], F32, name="q_raw%d" % o)
+            nc.sync.dma_start(raw[:], qT[0, o * 512:(o + 1) * 512, :].rearrange("(p j) w -> p j w", j=PACK))
+            q_raw.append(raw)
+
+        ks_pool = load_scale_pool("ks_pool", k_scales, nc.scalar)
+        cs_pool = load_scale_pool("cs_pool", c_scales, nc.gpsimd)
+
+        def load_word_pool(name, words):
+            pool_tile = held.tile([P, TOKENS], I32, name=name, align_bytes=64)
+            nc.sync.dma_start(pool_tile[:], words[0].rearrange("p t b -> p (t b)").bitcast(I32))
+            return pool_tile
+
+        kw_pool = load_word_pool("kw_pool", k_words)
+        cw_pool = load_word_pool("cw_pool", c_words)
+
+        v_pool = []
+        for e in range(E_BLOCKS):
+            if e == E_BLOCKS - 1:
+                og_sb = held.tile([P, Q_TILES, DV], F32, name="og_sb")
+                nc.sync.dma_start(og_sb[:], og[0].rearrange("(j p) e -> p j e", p=P))
+            vt = held.tile([P, TOKENS], F32, name="v_pool%d" % e, align_bytes=64)
+            nc.sync.dma_start(vt[:], vT[e * P:(e + 1) * P, :])
+            v_pool.append(vt)
+
+        ident = held.tile([P, P], F32, name="ident")
+        make_identity(nc, ident[:])
+
+        th_rows = held.tile([P, P], F32, name="th_rows")
+        nc.gpsimd.memset(th_rows[:], 0.0)
+        nc.gpsimd.dma_start(th_rows[0:Q_TILES, :], th[0, 0].rearrange("(j p) -> j p", p=P))
+        us_sb = held.tile([P, PACK], F32, name="us_sb")
+        nc.gpsimd.dma_start(us_sb[:], us[0].rearrange("(p t) one -> p (t one)", t=PACK))
+        th_bank = psum.tile([P, P], F32, name="th_bank", tag="vt")
+        nc.tensor.transpose(th_bank[:], th_rows[:], ident[:])
+        neg_th = held.tile([P, Q_TILES], F32, name="neg_th")
+        nc.scalar.activation(neg_th[:], th_bank[:, 0:Q_TILES], ACT.Copy, scale=-1.0)
+
+        def gather_scales(name, pool_tile):
+            first = held.tile([P, SLOTS], U8, name=name + "0", align_bytes=64)
+            second = held.tile([P, SLOTS], U8, name=name + "1", align_bytes=64)
+            nc.gpsimd.memset(second[:].bitcast(I32), 0)
+            nc.vector.tensor_copy(first[:], pool_tile[:].indirect(offsets[:]))
+            nc.gpsimd.dma_start(second[0:P - 16, :].bitcast(I32), first[16:P, :].bitcast(I32))
+            return [first, second]
+
+        ks = gather_scales("ks", ks_pool)
+        cs = gather_scales("cs", cs_pool)
+
+        q_codes = []
+        q_scales = []
+        for o in range(PASSES):
+            grouped = held.tile([P, NQ, PACK], BF16, name="q_grouped%d" % o, align_bytes=64)
+            dst = grouped[:].rearrange("p (c i) t -> p c t i", i=4)
+            src = q_raw[o][:].rearrange("p t (c i) -> p c t i", i=4)
+            if o == 0:
+                nc.scalar.copy(dst, src)
+            else:
+                nc.vector.tensor_copy(dst, src)
+            codes = held.tile([P, NQ], U32, name="q_codes%d" % o, align_bytes=64)
+            scales = held.tile([P, NQ], U8, name="q_scales%d" % o, align_bytes=64)
+            nc.vector.quantize_mx(out=codes[:].bitcast(FP8X4), scales=scales[:], in_=grouped[:].rearrange("p w j -> p (w j)"))
+            q_codes.append(codes)
+            q_scales.append(scales)
+
+        def gather_words(name, pool_tile):
+            both = held.tile([P, SLOTS], U32, name=name + "_both", align_bytes=64)
+            nc.vector.tensor_copy(both[:], pool_tile[:].bitcast(U32).indirect(offsets[:]))
+            parted = held.tile([P, PASSES, SLOTS], U16, name=name + "_parted", align_bytes=64)
+            nc.vector.tensor_copy(parted[:], both[:].bitcast(U16).rearrange("p (s o) -> p o s", o=PASSES))
+            return parted
+
+        kw = gather_words("kw", kw_pool)
+        cw = gather_words("cw", cw_pool)
+
+        def score_sigmoid(j, tag, words, scales):
+            cols = slice(j * P, (j + 1) * P)
+            bank = psum.tile([P, SLOTS], F32, name=tag, tag=tag)
+            for o in range(PASSES):
+                nc.tensor.matmul_mx(
+                    out=bank[:],
+                    lhsT=q_codes[o][:, cols].bitcast(FP8X4),
+                    lhsT_scale=q_scales[o][:, cols],
+                    rhs=words[:, o, :].bitcast(FP4X4),
+                    rhs_scale=scales[o][:],
+                    start=(o == 0),
+                    stop=(o == PASSES - 1),
+                )
+            sig = held.tile([P, PACK, P], F32, name="sig_%s%d" % (tag, j))
+            nc.scalar.activation(sig[:], bank[:].rearrange("p (s t) -> p t s", t=PACK), ACT.Sigmoid, bias=neg_th[:, j:j + 1])
+            return sig
+
+        sig_a = [score_sigmoid(j, "sa", kw, ks) for j in range(Q_TILES)]
+
+        def values_block(e):
+            picked = work.tile([P, SLOTS], BF16, name="v_picked", align_bytes=64)
+            nc.vector.tensor_copy(picked[:], v_pool[e][:].indirect(offsets[:]))
+            words = picked[:].bitcast(F32)
+            bank = psum.tile([P, 2, P], F32, name="v_bank", tag="vt")
+            for u in range(2):
+                nc.tensor.transpose(bank[:, u, :], words[:, u:2 * P:2], ident[:])
+            grouped = held.tile([P, P, PACK], BF16, name="v_grouped%d" % e, align_bytes=64)
+            nc.scalar.copy(grouped[:].bitcast(F32), bank[:].rearrange("p u e -> p e u"))
+            return grouped
+
+        def values_quantise(e, grouped):
+            codes = held.tile([P, P], U32, name="v_codes%d" % e, align_bytes=64)
+            scales = held.tile([P, P], U8, name="v_scales%d" % e, align_bytes=64)
+            nc.vector.quantize_mx(out=codes[:].bitcast(FP8X4), scales=scales[:], in_=grouped[:].rearrange("p w j -> p (w j)"))
+            return codes, scales
+
+        y_codes = []
+        y_scales = []
+        v_grouped = []
+        y_half = None
+        for j in range(Q_TILES):
+            sig_z = score_sigmoid(j, "sz", cw, cs)
+            if j < E_BLOCKS - 1:
+                v_grouped.append(values_block(j))
+            best = work.tile([P, PACK, P], F32, name="best")
+            nc.vector.tensor_tensor(best[:], sig_a[j][:], sig_z[:], ALU.max)
+            bank = psum.tile([P, PACK, P], F32, name="y_bank", tag="tr")
+            for t in range(PACK):
+                nc.tensor.transpose(bank[:, t, :], best[:, t, :], ident[:])
+            if j % 2 == 0:
+                y_half = held.tile([P, 2, P, PACK], BF16, name="y_half%d" % j, align_bytes=64)
+            nc.vector.tensor_tensor(
+                y_half[:, j % 2],
+                bank[:].rearrange("p t q -> p q t"),
+                us_sb[:].unsqueeze(1).to_broadcast([P, P, PACK]),
+                ALU.mult,
+            )
+            if j % 2 == 1:
+                codes = held.tile([P, 2 * P], U32, name="y_codes%d" % j, align_bytes=64)
+                scales = held.tile([P, 2 * P], U8, name="y_scales%d" % j, align_bytes=64)
+                nc.vector.quantize_mx(out=codes[:].bitcast(FP8X4), scales=scales[:], in_=y_half[:].rearrange("p h q t -> p (h q t)"))
+                for h in range(2):
+                    y_codes.append(codes[:, h * P:(h + 1) * P])
+                    y_scales.append(scales[:, h * P:(h + 1) * P])
+
+        out_view = out[0].rearrange("(j p) e -> p j e", p=P)
+
+        def finish_block(e, v_codes, v_scales):
+            cols = slice(e * P, (e + 1) * P)
+            gate = held.tile([P, Q_TILES, P], F32, name="gate%d" % e)
+            nc.scalar.activation(gate[:], og_sb[:, :, cols], ACT.Sigmoid)
+            bank = psum.tile([P, Q_TILES, P], F32, name="o_bank", tag=("sa", "sz")[e % 2])
+            for j in range(Q_TILES):
+                nc.tensor.matmul_mx(
+                    out=bank[:, j, :],
+                    lhsT=y_codes[j].bitcast(FP8X4),
+                    lhsT_scale=y_scales[j],
+                    rhs=v_codes[:].bitcast(FP8X4),
+                    rhs_scale=v_scales[:],
+                    start=True,
+                    stop=True,
+                )
+            result = held.tile([P, Q_TILES, P], F32, name="result%d" % e)
+            nc.vector.tensor_tensor(result[:], bank[:], gate[:], ALU.mult)
+            nc.sync.dma_start(out_view[:, :, cols], result[:])
+
+        v_mx = [values_quantise(e, v_grouped[e]) for e in range(E_BLOCKS - 1)]
+        last_grouped = values_block(E_BLOCKS - 1)
+        for e in range(E_BLOCKS - 1):
+            finish_block(e, *v_mx[e])
+        finish_block(E_BLOCKS - 1, *values_quantise(E_BLOCKS - 1, last_grouped))

@@ -25,6 +25,9 @@ PASSES = D // (P * PACK)
 Q_TILES = NQ // P
 E_BLOCKS = DV // P
 
+SLOT_BYTES = 4 * TOKENS
+CELL_BYTES = 4 * SLOTS
+
 FLOPS = 2 * 2 * SLOTS * D * NQ + 2 * NQ * SLOTS * DV
 
 
@@ -32,74 +35,74 @@ def tile_attend_at_proto_topk_kernel(tc, qT, k_words, k_scales, c_words, c_scale
     nc = tc.nc
     with ExitStack() as ctx:
         held = ctx.enter_context(tc.tile_pool(name="held", bufs=1))
-        work = ctx.enter_context(tc.tile_pool(name="work", bufs=2))
+        ring = ctx.enter_context(tc.tile_pool(name="ring", bufs=1))
+        work = ctx.enter_context(tc.tile_pool(name="work", bufs=1))
         psum = ctx.enter_context(tc.psum_pool(name="psum", bufs=2))
 
         offsets = held.tile([P, SLOTS // 16], U16, name="offsets")
         nc.sync.dma_start(offsets[:], offs)
 
-        warm_in = held.tile([P, 8], F32, name="warm_in")
+        def load_scale_pool(name, slot, scales, zeroing, queue):
+            pool_tile = ring.tile([P, TOKENS], U8, name=name, offset=slot * SLOT_BYTES, align_bytes=64)
+            zeroing.memset(pool_tile[:].bitcast(I32), 0)
+            queue.dma_start(pool_tile[0:P:4, :].bitcast(I32), scales.rearrange("o f t -> f o t").bitcast(I32))
+            return pool_tile
+
+        ks_pool = load_scale_pool("ks_pool", 4, k_scales, nc.gpsimd, nc.sync)
+        cs_pool = load_scale_pool("cs_pool", 2, c_scales, nc.vector, nc.scalar)
+
+        warm_in = ring.tile([P, 8], F32, name="warm_in", offset=0, align_bytes=64)
         warm_out = held.tile([P, 8], F32, name="warm_out")
         nc.vector.memset(warm_in[:], 0.0)
         nc.scalar.activation(warm_out[:], warm_in[:], ACT.Sigmoid)
 
-        def load_scale_pool(name, scales, queue):
-            pool_tile = held.tile([P, TOKENS], U8, name=name, align_bytes=64)
-            nc.vector.memset(pool_tile[:].bitcast(I32), 0)
-            rows = scales.rearrange("o (q r) t -> r q o t", r=4)
-            for r in range(4):
-                queue.dma_start(pool_tile[r:P:16, :].bitcast(I32), rows[r].bitcast(I32))
-            return pool_tile
-
-        q_raw = []
-        for o in range(PASSES):
-            raw = held.tile([P, PACK, NQ], F32, name="q_raw%d" % o)
-            nc.sync.dma_start(raw[:], qT[0, o * 512:(o + 1) * 512, :].rearrange("(p j) w -> p j w", j=PACK))
-            q_raw.append(raw)
-
-        ks_pool = load_scale_pool("ks_pool", k_scales, nc.scalar)
-        cs_pool = load_scale_pool("cs_pool", c_scales, nc.gpsimd)
-
-        def load_word_pool(name, words):
-            pool_tile = held.tile([P, TOKENS], I32, name=name, align_bytes=64)
-            nc.sync.dma_start(pool_tile[:], words[0].rearrange("p t b -> p (t b)").bitcast(I32))
-            return pool_tile
-
-        kw_pool = load_word_pool("kw_pool", k_words)
-        cw_pool = load_word_pool("cw_pool", c_words)
-
-        v_pool = []
-        for e in range(E_BLOCKS):
-            if e == E_BLOCKS - 1:
-                og_sb = held.tile([P, Q_TILES, DV], F32, name="og_sb")
-                nc.sync.dma_start(og_sb[:], og[0].rearrange("(j p) e -> p j e", p=P))
-            vt = held.tile([P, TOKENS], F32, name="v_pool%d" % e, align_bytes=64)
-            nc.sync.dma_start(vt[:], vT[e * P:(e + 1) * P, :])
-            v_pool.append(vt)
-
+        th_rows = ring.tile([P, P], F32, name="th_rows", offset=SLOT_BYTES, align_bytes=64)
+        nc.gpsimd.memset(th_rows[:], 0.0)
+        nc.scalar.dma_start(th_rows[0:Q_TILES, :], th[0, 0].rearrange("(j p) -> j p", p=P))
+        us_sb = held.tile([P, PACK], F32, name="us_sb")
         ident = held.tile([P, P], F32, name="ident")
         make_identity(nc, ident[:])
-
-        th_rows = held.tile([P, P], F32, name="th_rows")
-        nc.gpsimd.memset(th_rows[:], 0.0)
-        nc.gpsimd.dma_start(th_rows[0:Q_TILES, :], th[0, 0].rearrange("(j p) -> j p", p=P))
-        us_sb = held.tile([P, PACK], F32, name="us_sb")
-        nc.gpsimd.dma_start(us_sb[:], us[0].rearrange("(p t) one -> p (t one)", t=PACK))
         th_bank = psum.tile([P, P], F32, name="th_bank", tag="vt")
         nc.tensor.transpose(th_bank[:], th_rows[:], ident[:])
         neg_th = held.tile([P, Q_TILES], F32, name="neg_th")
         nc.scalar.activation(neg_th[:], th_bank[:, 0:Q_TILES], ACT.Copy, scale=-1.0)
 
-        def gather_scales(name, pool_tile):
-            first = held.tile([P, SLOTS], U8, name=name + "0", align_bytes=64)
-            second = held.tile([P, SLOTS], U8, name=name + "1", align_bytes=64)
-            nc.gpsimd.memset(second[:].bitcast(I32), 0)
-            nc.vector.tensor_copy(first[:], pool_tile[:].indirect(offsets[:]))
-            nc.gpsimd.dma_start(second[0:P - 16, :].bitcast(I32), first[16:P, :].bitcast(I32))
-            return [first, second]
+        q_raw = []
+        for o in range(PASSES):
+            raw = ring.tile([P, PACK, NQ], F32, name="q_raw%d" % o, offset=(3, 1)[o] * SLOT_BYTES, align_bytes=64)
+            nc.sync.dma_start(raw[:], qT[0, o * 512:(o + 1) * 512, :].rearrange("(p j) w -> p j w", j=PACK))
+            q_raw.append(raw)
 
-        ks = gather_scales("ks", ks_pool)
-        cs = gather_scales("cs", cs_pool)
+        nc.gpsimd.dma_start(us_sb[:], us[0].rearrange("(p t) one -> p (t one)", t=PACK))
+
+        def load_word_pool(name, words, slot):
+            pool_tile = ring.tile([P, TOKENS], I32, name=name, offset=slot * SLOT_BYTES, align_bytes=64)
+            nc.sync.dma_start(pool_tile[:], words[0].rearrange("p t b -> p (t b)").bitcast(I32))
+            return pool_tile
+
+        kw_pool = load_word_pool("kw_pool", k_words, 0)
+        cw_pool = load_word_pool("cw_pool", c_words, 2)
+
+        def gather_scales(name, pool_tile, queue):
+            picked = held.tile([P, SLOTS], U8, name=name + "_picked", align_bytes=64)
+            planes = held.tile([P, PASSES * SLOTS], U8, name=name + "_planes", align_bytes=64)
+            nc.gpsimd.memset(planes[:].bitcast(I32), 0)
+            nc.vector.tensor_copy(picked[:], pool_tile[:].indirect(offsets[:]))
+            for quad in range(4):
+                queue.dma_start(planes[32 * quad:32 * quad + 4, :].bitcast(I32), picked[32 * quad:32 * quad + 32:4, :].bitcast(I32))
+            return [planes[:, o * SLOTS:(o + 1) * SLOTS] for o in range(PASSES)]
+
+        ks = gather_scales("ks", ks_pool, nc.gpsimd)
+        cs = gather_scales("cs", cs_pool, nc.scalar)
+
+        def gather_words(name, pool_tile):
+            both = work.tile([P, SLOTS], U32, name=name + "_both", offset=0, align_bytes=64)
+            nc.vector.tensor_copy(both[:], pool_tile[:].bitcast(U32).indirect(offsets[:]))
+            parted = held.tile([P, PASSES, SLOTS], U16, name=name + "_parted", align_bytes=64)
+            nc.vector.tensor_copy(parted[:], both[:].bitcast(U16).rearrange("p (s o) -> p o s", o=PASSES))
+            return parted
+
+        kw = gather_words("kw", kw_pool)
 
         q_codes = []
         q_scales = []
@@ -117,37 +120,46 @@ def tile_attend_at_proto_topk_kernel(tc, qT, k_words, k_scales, c_words, c_scale
             q_codes.append(codes)
             q_scales.append(scales)
 
-        def gather_words(name, pool_tile):
-            both = held.tile([P, SLOTS], U32, name=name + "_both", align_bytes=64)
-            nc.vector.tensor_copy(both[:], pool_tile[:].bitcast(U32).indirect(offsets[:]))
-            parted = held.tile([P, PASSES, SLOTS], U16, name=name + "_parted", align_bytes=64)
-            nc.vector.tensor_copy(parted[:], both[:].bitcast(U16).rearrange("p (s o) -> p o s", o=PASSES))
-            return parted
-
-        kw = gather_words("kw", kw_pool)
         cw = gather_words("cw", cw_pool)
 
-        def score_sigmoid(j, tag, words, scales):
+        def load_values(e):
+            vt = ring.tile([P, TOKENS], F32, name="v_pool%d" % e, offset=(3, 0, 1, 3)[e] * SLOT_BYTES, align_bytes=64)
+            nc.sync.dma_start(vt[:], vT[e * P:(e + 1) * P, :])
+            return vt
+
+        v_pool = [load_values(e) for e in range(E_BLOCKS - 1)]
+
+        def score_pass(bank, j, o, words, scales):
             cols = slice(j * P, (j + 1) * P)
-            bank = psum.tile([P, SLOTS], F32, name=tag, tag=tag)
-            for o in range(PASSES):
-                nc.tensor.matmul_mx(
-                    out=bank[:],
-                    lhsT=q_codes[o][:, cols].bitcast(FP8X4),
-                    lhsT_scale=q_scales[o][:, cols],
-                    rhs=words[:, o, :].bitcast(FP4X4),
-                    rhs_scale=scales[o][:],
-                    start=(o == 0),
-                    stop=(o == PASSES - 1),
-                )
-            sig = held.tile([P, PACK, P], F32, name="sig_%s%d" % (tag, j))
+            nc.tensor.matmul_mx(
+                out=bank[:],
+                lhsT=q_codes[o][:, cols].bitcast(FP8X4),
+                lhsT_scale=q_scales[o][:, cols],
+                rhs=words[:, o, :].bitcast(FP4X4),
+                rhs_scale=scales[o],
+                start=(o == 0),
+                stop=(o == PASSES - 1),
+            )
+
+        def sigmoid_of(bank, j, name):
+            sig = held.tile([P, PACK, P], F32, name=name)
             nc.scalar.activation(sig[:], bank[:].rearrange("p (s t) -> p t s", t=PACK), ACT.Sigmoid, bias=neg_th[:, j:j + 1])
             return sig
 
-        sig_a = [score_sigmoid(j, "sa", kw, ks) for j in range(Q_TILES)]
+        a_banks = [psum.tile([P, SLOTS], F32, name="a_bank", tag="score", bufs=4) for j in range(Q_TILES)]
+        for o in range(PASSES):
+            for j in range(Q_TILES):
+                score_pass(a_banks[j], j, o, kw, ks)
+        sig_a = [sigmoid_of(a_banks[j], j, "sig_a%d" % j) for j in range(Q_TILES)]
+        sig_z = []
+        for j in range(Q_TILES):
+            z_bank = psum.tile([P, SLOTS], F32, name="z_bank", tag="score", bufs=4)
+            for o in range(PASSES):
+                score_pass(z_bank, j, o, cw, cs)
+            sig_z.append(sigmoid_of(z_bank, j, "sig_z%d" % j))
 
         def values_block(e):
-            picked = work.tile([P, SLOTS], BF16, name="v_picked", align_bytes=64)
+            picked = work.tile([P, SLOTS], BF16, name="v_picked%d" % e, offset=(0, 1, 3, 6)[e] * CELL_BYTES, align_bytes=64)
             nc.vector.tensor_copy(picked[:], v_pool[e][:].indirect(offsets[:]))
             words = picked[:].bitcast(F32)
             bank = psum.tile([P, 2, P], F32, name="v_bank", tag="vt")
@@ -168,16 +180,16 @@ def tile_attend_at_proto_topk_kernel(tc, qT, k_words, k_scales, c_words, c_scale
         v_grouped = []
         y_half = None
         for j in range(Q_TILES):
-            sig_z = score_sigmoid(j, "sz", cw, cs)
-            if j < E_BLOCKS - 1:
-                v_grouped.append(values_block(j))
-            best = work.tile([P, PACK, P], F32, name="best")
-            nc.vector.tensor_tensor(best[:], sig_a[j][:], sig_z[:], ALU.max)
+            if j == 0:
+                v_grouped.append(values_block(0))
+            best = work.tile([P, PACK, P], F32, name="best%d" % j, offset=(1 + j) * CELL_BYTES, align_bytes=64)
+            nc.vector.tensor_tensor(best[:], sig_a[j][:], sig_z[j][:], ALU.max)
             bank = psum.tile([P, PACK, P], F32, name="y_bank", tag="tr")
             for t in range(PACK):
                 nc.tensor.transpose(bank[:, t, :], best[:, t, :], ident[:])
             if j % 2 == 0:
-                y_half = held.tile([P, 2, P, PACK], BF16, name="y_half%d" % j, align_bytes=64)
+                v_grouped.append(values_block(1 + j // 2))
+                y_half = work.tile([P, 2, P, PACK], BF16, name="y_half%d" % j, offset=(5 + j // 2) * CELL_BYTES, align_bytes=64)
             nc.vector.tensor_tensor(
                 y_half[:, j % 2],
                 bank[:].rearrange("p t q -> p q t"),
@@ -192,13 +204,16 @@ def tile_attend_at_proto_topk_kernel(tc, qT, k_words, k_scales, c_words, c_scale
                     y_codes.append(codes[:, h * P:(h + 1) * P])
                     y_scales.append(scales[:, h * P:(h + 1) * P])
 
+        og_sb = ring.tile([P, Q_TILES, DV], F32, name="og_sb", offset=2 * SLOT_BYTES, align_bytes=64)
+        nc.sync.dma_start(og_sb[:], og[0].rearrange("(j p) e -> p j e", p=P))
+        v_pool.append(load_values(E_BLOCKS - 1))
         out_view = out[0].rearrange("(j p) e -> p j e", p=P)
 
         def finish_block(e, v_codes, v_scales):
             cols = slice(e * P, (e + 1) * P)
             gate = held.tile([P, Q_TILES, P], F32, name="gate%d" % e)
             nc.scalar.activation(gate[:], og_sb[:, :, cols], ACT.Sigmoid)
-            bank = psum.tile([P, Q_TILES, P], F32, name="o_bank", tag=("sa", "sz")[e % 2])
+            bank = psum.tile([P, Q_TILES, P], F32, name="o_bank", tag="score", bufs=4)
             for j in range(Q_TILES):
                 nc.tensor.matmul_mx(
                     out=bank[:, j, :],

@@ -49,17 +49,16 @@ def tile_attend_at_proto_topk_kernel(tc, qT, k_words, k_scales, c_words, c_scale
             return pool_tile
 
         ks_pool = load_scale_pool("ks_pool", 4, k_scales, nc.gpsimd, nc.sync)
-        cs_pool = load_scale_pool("cs_pool", 2, c_scales, nc.vector, nc.scalar)
+        cs_pool = load_scale_pool("cs_pool", 2, c_scales, nc.vector, nc.sync)
 
         warm_in = ring.tile([P, 8], F32, name="warm_in", offset=0, align_bytes=64)
-        warm_out = held.tile([P, 8], F32, name="warm_out")
+        warm_out = ring.tile([P, 8], F32, name="warm_out", offset=SLOT_BYTES, align_bytes=64)
         nc.vector.memset(warm_in[:], 0.0)
         nc.scalar.activation(warm_out[:], warm_in[:], ACT.Sigmoid)
 
-        th_rows = ring.tile([P, P], F32, name="th_rows", offset=SLOT_BYTES, align_bytes=64)
+        th_rows = ring.tile([P, P], F32, name="th_rows", offset=5 * SLOT_BYTES, align_bytes=64)
         nc.gpsimd.memset(th_rows[:], 0.0)
-        nc.scalar.dma_start(th_rows[0:Q_TILES, :], th[0, 0].rearrange("(j p) -> j p", p=P))
-        us_sb = held.tile([P, PACK], F32, name="us_sb")
+        nc.sync.dma_start(th_rows[0:Q_TILES, :], th[0, 0].rearrange("(j p) -> j p", p=P))
         ident = held.tile([P, P], F32, name="ident")
         make_identity(nc, ident[:])
         th_bank = psum.tile([P, P], F32, name="th_bank", tag="vt")
@@ -67,21 +66,21 @@ def tile_attend_at_proto_topk_kernel(tc, qT, k_words, k_scales, c_words, c_scale
         neg_th = held.tile([P, Q_TILES], F32, name="neg_th")
         nc.scalar.activation(neg_th[:], th_bank[:, 0:Q_TILES], ACT.Copy, scale=-1.0)
 
-        q_raw = []
-        for o in range(PASSES):
-            raw = ring.tile([P, PACK, NQ], F32, name="q_raw%d" % o, offset=(3, 1)[o] * SLOT_BYTES, align_bytes=64)
-            nc.sync.dma_start(raw[:], qT[0, o * 512:(o + 1) * 512, :].rearrange("(p j) w -> p j w", j=PACK))
-            q_raw.append(raw)
-
-        nc.gpsimd.dma_start(us_sb[:], us[0].rearrange("(p t) one -> p (t one)", t=PACK))
-
         def load_word_pool(name, words, slot):
             pool_tile = ring.tile([P, TOKENS], I32, name=name, offset=slot * SLOT_BYTES, align_bytes=64)
             nc.sync.dma_start(pool_tile[:], words[0].rearrange("p t b -> p (t b)").bitcast(I32))
             return pool_tile
 
-        kw_pool = load_word_pool("kw_pool", k_words, 0)
-        cw_pool = load_word_pool("cw_pool", c_words, 2)
+        q_raw = []
+        for o in range(PASSES):
+            if o == 1:
+                kw_pool = load_word_pool("kw_pool", k_words, 0)
+            raw = ring.tile([P, PACK, NQ], F32, name="q_raw%d" % o, offset=(3, 1)[o] * SLOT_BYTES, align_bytes=64)
+            nc.sync.dma_start(raw[:], qT[0, o * 512:(o + 1) * 512, :].rearrange("(p j) w -> p j w", j=PACK))
+            q_raw.append(raw)
+
+        us_sb = ring.tile([P, PACK], F32, name="us_sb", offset=5 * SLOT_BYTES, align_bytes=64)
+        nc.sync.dma_start(us_sb[:], us[0].rearrange("(p t) one -> p (t one)", t=PACK))
 
         def gather_scales(name, pool_tile, queue):
             picked = held.tile([P, SLOTS], U8, name=name + "_picked", align_bytes=64)
@@ -92,42 +91,47 @@ def tile_attend_at_proto_topk_kernel(tc, qT, k_words, k_scales, c_words, c_scale
                 queue.dma_start(planes[32 * quad:32 * quad + 4, :].bitcast(I32), picked[32 * quad:32 * quad + 32:4, :].bitcast(I32))
             return [planes[:, o * SLOTS:(o + 1) * SLOTS] for o in range(PASSES)]
 
-        ks = gather_scales("ks", ks_pool, nc.gpsimd)
-        cs = gather_scales("cs", cs_pool, nc.scalar)
+        ks = gather_scales("ks", ks_pool, nc.sync)
+        cw_pool = load_word_pool("cw_pool", c_words, 4)
+        cs = gather_scales("cs", cs_pool, nc.sync)
 
-        def gather_words(name, pool_tile):
-            both = work.tile([P, SLOTS], U32, name=name + "_both", offset=0, align_bytes=64)
+        def gather_words(name, pool_tile, cell):
+            both = work.tile([P, SLOTS], U32, name=name + "_both", offset=cell * CELL_BYTES, align_bytes=64)
             nc.vector.tensor_copy(both[:], pool_tile[:].bitcast(U32).indirect(offsets[:]))
             parted = held.tile([P, PASSES, SLOTS], U16, name=name + "_parted", align_bytes=64)
             nc.vector.tensor_copy(parted[:], both[:].bitcast(U16).rearrange("p (s o) -> p o s", o=PASSES))
             return parted
 
-        kw = gather_words("kw", kw_pool)
+        kw = gather_words("kw", kw_pool, 0)
 
         q_codes = []
         q_scales = []
         for o in range(PASSES):
-            grouped = held.tile([P, NQ, PACK], BF16, name="q_grouped%d" % o, align_bytes=64)
+            grouped = work.tile([P, NQ, PACK], BF16, name="q_grouped%d" % o, offset=(13, 7)[o] * CELL_BYTES, align_bytes=64)
             dst = grouped[:].rearrange("p (c i) t -> p c t i", i=4)
             src = q_raw[o][:].rearrange("p t (c i) -> p c t i", i=4)
             if o == 0:
                 nc.scalar.copy(dst, src)
             else:
-                nc.vector.tensor_copy(dst, src)
+                nc.vector.tensor_copy(dst[:, :88], src[:, :88])
+                nc.scalar.copy(dst[:, 88:], src[:, 88:])
             codes = held.tile([P, NQ], U32, name="q_codes%d" % o, align_bytes=64)
             scales = held.tile([P, NQ], U8, name="q_scales%d" % o, align_bytes=64)
             nc.vector.quantize_mx(out=codes[:].bitcast(FP8X4), scales=scales[:], in_=grouped[:].rearrange("p w j -> p (w j)"))
             q_codes.append(codes)
             q_scales.append(scales)
 
-        cw = gather_words("cw", cw_pool)
+        cw = gather_words("cw", cw_pool, 7)
 
         def load_values(e):
-            vt = ring.tile([P, TOKENS], F32, name="v_pool%d" % e, offset=(3, 0, 1, 3)[e] * SLOT_BYTES, align_bytes=64)
+            vt = ring.tile([P, TOKENS], F32, name="v_pool%d" % e, offset=(2, 3, 0, 4)[e] * SLOT_BYTES, align_bytes=64)
             nc.sync.dma_start(vt[:], vT[e * P:(e + 1) * P, :])
             return vt
 
         v_pool = [load_values(e) for e in range(E_BLOCKS - 1)]
+        og_sb = ring.tile([P, Q_TILES, DV], F32, name="og_sb", offset=SLOT_BYTES, align_bytes=64)
+        nc.sync.dma_start(og_sb[:], og[0].rearrange("(j p) e -> p j e", p=P))
+        v_pool.append(load_values(E_BLOCKS - 1))
 
         def score_pass(bank, j, o, words, scales):
             cols = slice(j * P, (j + 1) * P)
@@ -141,8 +145,8 @@ def tile_attend_at_proto_topk_kernel(tc, qT, k_words, k_scales, c_words, c_scale
                 stop=(o == PASSES - 1),
             )
 
-        def sigmoid_of(bank, j, name):
-            sig = held.tile([P, PACK, P], F32, name=name)
+        def sigmoid_of(bank, j, name, cell):
+            sig = work.tile([P, PACK, P], F32, name=name, offset=cell * CELL_BYTES, align_bytes=64)
             nc.scalar.activation(sig[:], bank[:].rearrange("p (s t) -> p t s", t=PACK), ACT.Sigmoid, bias=neg_th[:, j:j + 1])
             return sig
 
@@ -150,17 +154,22 @@ def tile_attend_at_proto_topk_kernel(tc, qT, k_words, k_scales, c_words, c_scale
         for o in range(PASSES):
             for j in range(Q_TILES):
                 score_pass(a_banks[j], j, o, kw, ks)
-        sig_a = [sigmoid_of(a_banks[j], j, "sig_a%d" % j) for j in range(Q_TILES)]
+        sig_a = [sigmoid_of(a_banks[j], j, "sig_a%d" % j, 9 + j) for j in range(Q_TILES)]
         sig_z = []
         for j in range(Q_TILES):
             z_bank = psum.tile([P, SLOTS], F32, name="z_bank", tag="score", bufs=4)
             for o in range(PASSES):
                 score_pass(z_bank, j, o, cw, cs)
-            sig_z.append(sigmoid_of(z_bank, j, "sig_z%d" % j))
+            sig_z.append(sigmoid_of(z_bank, j, "sig_z%d" % j, 15 + j))
 
         def values_block(e):
-            picked = work.tile([P, SLOTS], BF16, name="v_picked%d" % e, offset=(0, 1, 3, 6)[e] * CELL_BYTES, align_bytes=64)
-            nc.vector.tensor_copy(picked[:], v_pool[e][:].indirect(offsets[:]))
+            picked = work.tile([P, SLOTS], BF16, name="v_picked%d" % e, offset=(7, 0, 3, 6)[e] * CELL_BYTES, align_bytes=64)
+            if e == 1:
+                rounded = work.tile([P, TOKENS], BF16, name="v_rounded", offset=9 * CELL_BYTES, align_bytes=64)
+                nc.scalar.activation(rounded[:], v_pool[e][:], ACT.Copy)
+                nc.scalar.activation(picked[:], rounded[:].indirect(offsets[:]), ACT.Copy)
+            else:
+                nc.vector.tensor_copy(picked[:], v_pool[e][:].indirect(offsets[:]))
             words = picked[:].bitcast(F32)
             bank = psum.tile([P, 2, P], F32, name="v_bank", tag="vt")
             for u in range(2):
@@ -175,9 +184,15 @@ def tile_attend_at_proto_topk_kernel(tc, qT, k_words, k_scales, c_words, c_scale
             nc.vector.quantize_mx(out=codes[:].bitcast(FP8X4), scales=scales[:], in_=grouped[:].rearrange("p w j -> p (w j)"))
             return codes, scales
 
+        def gate_block(e):
+            gate = work.tile([P, Q_TILES, P], F32, name="gate%d" % e, offset=(9 + e) * CELL_BYTES, align_bytes=64)
+            nc.scalar.activation(gate[:], og_sb[:, :, e * P:(e + 1) * P], ACT.Sigmoid)
+            return gate
+
         y_codes = []
         y_scales = []
         v_grouped = []
+        v_mx = []
         y_half = None
         for j in range(Q_TILES):
             if j == 0:
@@ -187,8 +202,9 @@ def tile_attend_at_proto_topk_kernel(tc, qT, k_words, k_scales, c_words, c_scale
             bank = psum.tile([P, PACK, P], F32, name="y_bank", tag="tr")
             for t in range(PACK):
                 nc.tensor.transpose(bank[:, t, :], best[:, t, :], ident[:])
+            if j in (1, 2):
+                v_grouped.append(values_block(j))
             if j % 2 == 0:
-                v_grouped.append(values_block(1 + j // 2))
                 y_half = work.tile([P, 2, P, PACK], BF16, name="y_half%d" % j, offset=(5 + j // 2) * CELL_BYTES, align_bytes=64)
             nc.vector.tensor_tensor(
                 y_half[:, j % 2],
@@ -196,6 +212,11 @@ def tile_attend_at_proto_topk_kernel(tc, qT, k_words, k_scales, c_words, c_scale
                 us_sb[:].unsqueeze(1).to_broadcast([P, P, PACK]),
                 ALU.mult,
             )
+            if j == 1:
+                v_mx.append(values_quantise(0, v_grouped[0]))
+            if j == 3:
+                gates = [gate_block(e) for e in range(E_BLOCKS)]
+                v_mx.extend(values_quantise(e, v_grouped[e]) for e in (1, 2))
             if j % 2 == 1:
                 codes = held.tile([P, 2 * P], U32, name="y_codes%d" % j, align_bytes=64)
                 scales = held.tile([P, 2 * P], U8, name="y_scales%d" % j, align_bytes=64)
@@ -204,15 +225,10 @@ def tile_attend_at_proto_topk_kernel(tc, qT, k_words, k_scales, c_words, c_scale
                     y_codes.append(codes[:, h * P:(h + 1) * P])
                     y_scales.append(scales[:, h * P:(h + 1) * P])
 
-        og_sb = ring.tile([P, Q_TILES, DV], F32, name="og_sb", offset=2 * SLOT_BYTES, align_bytes=64)
-        nc.sync.dma_start(og_sb[:], og[0].rearrange("(j p) e -> p j e", p=P))
-        v_pool.append(load_values(E_BLOCKS - 1))
         out_view = out[0].rearrange("(j p) e -> p j e", p=P)
 
         def finish_block(e, v_codes, v_scales):
             cols = slice(e * P, (e + 1) * P)
-            gate = held.tile([P, Q_TILES, P], F32, name="gate%d" % e)
-            nc.scalar.activation(gate[:], og_sb[:, :, cols], ACT.Sigmoid)
             bank = psum.tile([P, Q_TILES, P], F32, name="o_bank", tag="score", bufs=4)
             for j in range(Q_TILES):
                 nc.tensor.matmul_mx(
@@ -224,11 +240,10 @@ def tile_attend_at_proto_topk_kernel(tc, qT, k_words, k_scales, c_words, c_scale
                     start=True,
                     stop=True,
                 )
-            result = held.tile([P, Q_TILES, P], F32, name="result%d" % e)
-            nc.vector.tensor_tensor(result[:], bank[:], gate[:], ALU.mult)
+            result = ring.tile([P, Q_TILES, P], F32, name="result%d" % e, offset=4 * SLOT_BYTES + e * CELL_BYTES, align_bytes=64)
+            nc.vector.tensor_tensor(result[:], bank[:], gates[e][:], ALU.mult)
             nc.sync.dma_start(out_view[:, :, cols], result[:])
 
-        v_mx = [values_quantise(e, v_grouped[e]) for e in range(E_BLOCKS - 1)]
         last_grouped = values_block(E_BLOCKS - 1)
         for e in range(E_BLOCKS - 1):
             finish_block(e, *v_mx[e])

@@ -163,9 +163,12 @@ def tile_attend_at_proto_topk_kernel(tc, qT, k_words, k_scales, c_words, c_scale
             sig_z.append(sigmoid_of(z_bank, j, "sig_z%d" % j, 15 + j))
 
         def values_block(e):
-            picked = work.tile([P, SLOTS], BF16, name="v_picked%d" % e, offset=(7, 0, 3, 6)[e] * CELL_BYTES, align_bytes=64)
+            if e == 3:
+                picked = ring.tile([P, SLOTS], BF16, name="v_picked3", offset=2 * SLOT_BYTES + 3 * CELL_BYTES, align_bytes=64)
+            else:
+                picked = work.tile([P, SLOTS], BF16, name="v_picked%d" % e, offset=(7, 0, 18)[e] * CELL_BYTES, align_bytes=64)
             if e == 1:
-                rounded = work.tile([P, TOKENS], BF16, name="v_rounded", offset=9 * CELL_BYTES, align_bytes=64)
+                rounded = work.tile([P, TOKENS], BF16, name="v_rounded", offset=8 * CELL_BYTES, align_bytes=64)
                 nc.scalar.activation(rounded[:], v_pool[e][:], ACT.Copy)
                 nc.scalar.activation(picked[:], rounded[:].indirect(offsets[:]), ACT.Copy)
             else:
@@ -174,18 +177,19 @@ def tile_attend_at_proto_topk_kernel(tc, qT, k_words, k_scales, c_words, c_scale
             bank = psum.tile([P, 2, P], F32, name="v_bank", tag="vt")
             for u in range(2):
                 nc.tensor.transpose(bank[:, u, :], words[:, u:2 * P:2], ident[:])
-            grouped = held.tile([P, P, PACK], BF16, name="v_grouped%d" % e, align_bytes=64)
+            grouped = ring.tile([P, P, PACK], BF16, name="v_grouped%d" % e, offset=(SLOT_BYTES if e == 3 else 6 * SLOT_BYTES + e * 1024), align_bytes=64)
             nc.scalar.copy(grouped[:].bitcast(F32), bank[:].rearrange("p u e -> p e u"))
             return grouped
 
         def values_quantise(e, grouped):
-            codes = held.tile([P, P], U32, name="v_codes%d" % e, align_bytes=64)
-            scales = held.tile([P, P], U8, name="v_scales%d" % e, align_bytes=64)
+            home = 5 * SLOT_BYTES + 512 if e == 0 else 4 * SLOT_BYTES + 3 * CELL_BYTES + (e - 1) * 640
+            codes = ring.tile([P, P], U32, name="v_codes%d" % e, offset=home, align_bytes=64)
+            scales = ring.tile([P, P], U8, name="v_scales%d" % e, offset=home + 512, align_bytes=64)
             nc.vector.quantize_mx(out=codes[:].bitcast(FP8X4), scales=scales[:], in_=grouped[:].rearrange("p w j -> p (w j)"))
             return codes, scales
 
         def gate_block(e):
-            gate = work.tile([P, Q_TILES, P], F32, name="gate%d" % e, offset=(9 + e) * CELL_BYTES, align_bytes=64)
+            gate = work.tile([P, Q_TILES, P], F32, name="gate%d" % e, offset=(8 + e) * CELL_BYTES, align_bytes=64)
             nc.scalar.activation(gate[:], og_sb[:, :, e * P:(e + 1) * P], ACT.Sigmoid)
             return gate
 
@@ -197,15 +201,18 @@ def tile_attend_at_proto_topk_kernel(tc, qT, k_words, k_scales, c_words, c_scale
         for j in range(Q_TILES):
             if j == 0:
                 v_grouped.append(values_block(0))
-            best = work.tile([P, PACK, P], F32, name="best%d" % j, offset=(1 + j) * CELL_BYTES, align_bytes=64)
+            if j == 2:
+                v_grouped.append(values_block(1))
+            best = ring.tile([P, PACK, P], F32, name="best%d" % j, offset=2 * SLOT_BYTES + j * CELL_BYTES, align_bytes=64)
             nc.vector.tensor_tensor(best[:], sig_a[j][:], sig_z[j][:], ALU.max)
             bank = psum.tile([P, PACK, P], F32, name="y_bank", tag="tr")
             for t in range(PACK):
                 nc.tensor.transpose(bank[:, t, :], best[:, t, :], ident[:])
-            if j in (1, 2):
-                v_grouped.append(values_block(j))
-            if j % 2 == 0:
-                y_half = work.tile([P, 2, P, PACK], BF16, name="y_half%d" % j, offset=(5 + j // 2) * CELL_BYTES, align_bytes=64)
+            if j == 0:
+                y_half = work.tile([P, 2, P, PACK], BF16, name="y_half0", offset=16 * CELL_BYTES, align_bytes=64)
+            if j == 2:
+                v_grouped.append(values_block(2))
+                y_half = ring.tile([P, 2, P, PACK], BF16, name="y_half1", offset=CELL_BYTES, align_bytes=64)
             nc.vector.tensor_tensor(
                 y_half[:, j % 2],
                 bank[:].rearrange("p t q -> p q t"),
@@ -216,7 +223,6 @@ def tile_attend_at_proto_topk_kernel(tc, qT, k_words, k_scales, c_words, c_scale
                 v_mx.append(values_quantise(0, v_grouped[0]))
             if j == 3:
                 gates = [gate_block(e) for e in range(E_BLOCKS)]
-                v_mx.extend(values_quantise(e, v_grouped[e]) for e in (1, 2))
             if j % 2 == 1:
                 codes = held.tile([P, 2 * P], U32, name="y_codes%d" % j, align_bytes=64)
                 scales = held.tile([P, 2 * P], U8, name="y_scales%d" % j, align_bytes=64)
@@ -240,11 +246,11 @@ def tile_attend_at_proto_topk_kernel(tc, qT, k_words, k_scales, c_words, c_scale
                     start=True,
                     stop=True,
                 )
-            result = ring.tile([P, Q_TILES, P], F32, name="result%d" % e, offset=4 * SLOT_BYTES + e * CELL_BYTES, align_bytes=64)
+            result = ring.tile([P, Q_TILES, P], F32, name="result%d" % e, offset=(4 * SLOT_BYTES + e * CELL_BYTES if e < 3 else 0), align_bytes=64)
             nc.vector.tensor_tensor(result[:], bank[:], gates[e][:], ALU.mult)
             nc.sync.dma_start(out_view[:, :, cols], result[:])
 
-        last_grouped = values_block(E_BLOCKS - 1)
-        for e in range(E_BLOCKS - 1):
+        v_grouped.append(values_block(E_BLOCKS - 1))
+        v_mx.extend(values_quantise(e, v_grouped[e]) for e in range(1, E_BLOCKS))
+        for e in range(E_BLOCKS):
             finish_block(e, *v_mx[e])
-        finish_block(E_BLOCKS - 1, *values_quantise(E_BLOCKS - 1, last_grouped))

@@ -15,18 +15,34 @@ ACT = mybir.ActivationFunctionType
 ALU = mybir.AluOpType
 
 P = 128
+PACK = 4
+QUAD = 32
 SLOTS = 512
 TOKENS = 2048
 D = 1024
 NQ = 512
 DV = 512
-PACK = 4
 PASSES = D // (P * PACK)
 Q_TILES = NQ // P
 E_BLOCKS = DV // P
+HALF = DV // 2
+SCORE_BANKS = 4
 
-SLOT_BYTES = 4 * TOKENS
-CELL_BYTES = 4 * SLOTS
+Q_SPLIT = 88
+SCALAR_BLOCK = 1
+
+CELL = 4 * SLOTS
+BAY = 4 * CELL
+BAY_K = 0
+BAY_Q1 = BAY
+BAY_CS = 2 * BAY
+BAY_Q0 = 3 * BAY
+BAY_C = 4 * BAY
+AT_TH = 5 * BAY
+AT_Q1_GROUPED = AT_TH + CELL
+AT_SIG_A = AT_Q1_GROUPED + 2 * CELL
+AT_SIG_Z = AT_SIG_A + Q_TILES * CELL
+AT_ROUNDED = AT_SIG_A - CELL
 
 FLOPS = 2 * 2 * SLOTS * D * NQ + 2 * NQ * SLOTS * DV
 
@@ -35,103 +51,114 @@ def tile_attend_at_proto_topk_kernel(tc, qT, k_words, k_scales, c_words, c_scale
     nc = tc.nc
     with ExitStack() as ctx:
         held = ctx.enter_context(tc.tile_pool(name="held", bufs=1))
-        ring = ctx.enter_context(tc.tile_pool(name="ring", bufs=1))
-        work = ctx.enter_context(tc.tile_pool(name="work", bufs=1))
+        shared = ctx.enter_context(tc.tile_pool(name="shared", bufs=1))
         psum = ctx.enter_context(tc.psum_pool(name="psum", bufs=2))
+
+        def own(name, shape, dtype):
+            return held.tile(shape, dtype, name=name, align_bytes=64)
+
+        def placed(name, shape, dtype, at):
+            return shared.tile(shape, dtype, name=name, offset=at, align_bytes=64)
+
+        def quantise(codes, scales, grouped):
+            nc.vector.quantize_mx(out=codes.bitcast(FP8X4), scales=scales, in_=grouped)
 
         offsets = held.tile([P, SLOTS // 16], U16, name="offsets")
         nc.sync.dma_start(offsets[:], offs)
 
-        def load_scale_pool(name, slot, scales, zeroing, queue):
-            pool_tile = ring.tile([P, TOKENS], U8, name=name, offset=slot * SLOT_BYTES, align_bytes=64)
+
+        def load_scale_pool(name, at, scales, zeroing):
+            pool_tile = placed(name, [P, TOKENS], U8, at)
             zeroing.memset(pool_tile[:].bitcast(I32), 0)
-            queue.dma_start(pool_tile[0:P:4, :].bitcast(I32), scales.rearrange("o f t -> f o t").bitcast(I32))
+            nc.sync.dma_start(pool_tile[0:P:4, :].bitcast(I32), scales.rearrange("o f t -> f o t").bitcast(I32))
             return pool_tile
 
-        ks_pool = load_scale_pool("ks_pool", 4, k_scales, nc.gpsimd, nc.sync)
-        cs_pool = load_scale_pool("cs_pool", 2, c_scales, nc.vector, nc.sync)
+        ks_pool = load_scale_pool("ks_pool", BAY_C, k_scales, nc.gpsimd)
+        cs_pool = load_scale_pool("cs_pool", BAY_CS, c_scales, nc.vector)
 
-        warm_in = ring.tile([P, 8], F32, name="warm_in", offset=0, align_bytes=64)
-        warm_out = ring.tile([P, 8], F32, name="warm_out", offset=SLOT_BYTES, align_bytes=64)
+        warm_in = placed("warm_in", [P, 8], F32, BAY_K)
+        warm_out = placed("warm_out", [P, 8], F32, BAY_Q1)
         nc.vector.memset(warm_in[:], 0.0)
         nc.scalar.activation(warm_out[:], warm_in[:], ACT.Sigmoid)
 
-        th_rows = ring.tile([P, P], F32, name="th_rows", offset=5 * SLOT_BYTES, align_bytes=64)
+        th_rows = placed("th_rows", [P, P], F32, AT_TH)
         nc.gpsimd.memset(th_rows[:], 0.0)
         nc.sync.dma_start(th_rows[0:Q_TILES, :], th[0, 0].rearrange("(j p) -> j p", p=P))
-        ident = held.tile([P, P], F32, name="ident")
+        ident = own("ident", [P, P], F32)
         make_identity(nc, ident[:])
-        th_bank = psum.tile([P, P], F32, name="th_bank", tag="vt")
+        th_bank = psum.tile([P, P], F32, name="th_bank", tag="turned_values")
         nc.tensor.transpose(th_bank[:], th_rows[:], ident[:])
-        neg_th = held.tile([P, Q_TILES], F32, name="neg_th")
+        neg_th = own("neg_th", [P, Q_TILES], F32)
         nc.scalar.activation(neg_th[:], th_bank[:, 0:Q_TILES], ACT.Copy, scale=-1.0)
 
-        def load_word_pool(name, words, slot):
-            pool_tile = ring.tile([P, TOKENS], I32, name=name, offset=slot * SLOT_BYTES, align_bytes=64)
+        def load_word_pool(name, at, words):
+            pool_tile = placed(name, [P, TOKENS], I32, at)
             nc.sync.dma_start(pool_tile[:], words[0].rearrange("p t b -> p (t b)").bitcast(I32))
             return pool_tile
 
-        q_raw = []
-        for o in range(PASSES):
-            if o == 1:
-                kw_pool = load_word_pool("kw_pool", k_words, 0)
-            raw = ring.tile([P, PACK, NQ], F32, name="q_raw%d" % o, offset=(3, 1)[o] * SLOT_BYTES, align_bytes=64)
-            nc.sync.dma_start(raw[:], qT[0, o * 512:(o + 1) * 512, :].rearrange("(p j) w -> p j w", j=PACK))
-            q_raw.append(raw)
+        def load_queries(o, at):
+            raw = placed("q_raw%d" % o, [P, PACK, NQ], F32, at)
+            rows = qT[0, o * P * PACK:(o + 1) * P * PACK, :]
+            nc.sync.dma_start(raw[:], rows.rearrange("(p t) q -> p t q", t=PACK))
+            return raw
 
-        us_sb = ring.tile([P, PACK], F32, name="us_sb", offset=5 * SLOT_BYTES, align_bytes=64)
+        q_raw = [load_queries(0, BAY_Q0)]
+        kw_pool = load_word_pool("kw_pool", BAY_K, k_words)
+        q_raw.append(load_queries(1, BAY_Q1))
+
+        us_sb = placed("us_sb", [P, PACK], F32, AT_TH)
         nc.sync.dma_start(us_sb[:], us[0].rearrange("(p t) one -> p (t one)", t=PACK))
 
-        def gather_scales(name, pool_tile, queue):
-            picked = held.tile([P, SLOTS], U8, name=name + "_picked", align_bytes=64)
-            planes = held.tile([P, PASSES * SLOTS], U8, name=name + "_planes", align_bytes=64)
+
+        def gather_scales(name, pool_tile):
+            picked = own(name + "_picked", [P, SLOTS], U8)
+            planes = own(name + "_planes", [P, PASSES * SLOTS], U8)
             nc.gpsimd.memset(planes[:].bitcast(I32), 0)
             nc.vector.tensor_copy(picked[:], pool_tile[:].indirect(offsets[:]))
-            for quad in range(4):
-                queue.dma_start(planes[32 * quad:32 * quad + 4, :].bitcast(I32), picked[32 * quad:32 * quad + 32:4, :].bitcast(I32))
+            for first in range(0, P, QUAD):
+                nc.sync.dma_start(planes[first:first + PACK, :].bitcast(I32), picked[first:first + QUAD:4, :].bitcast(I32))
             return [planes[:, o * SLOTS:(o + 1) * SLOTS] for o in range(PASSES)]
 
-        ks = gather_scales("ks", ks_pool, nc.sync)
-        cw_pool = load_word_pool("cw_pool", c_words, 4)
-        cs = gather_scales("cs", cs_pool, nc.sync)
-
-        def gather_words(name, pool_tile, cell):
-            both = work.tile([P, SLOTS], U32, name=name + "_both", offset=cell * CELL_BYTES, align_bytes=64)
+        def gather_words(name, pool_tile, both):
             nc.vector.tensor_copy(both[:], pool_tile[:].bitcast(U32).indirect(offsets[:]))
-            parted = held.tile([P, PASSES, SLOTS], U16, name=name + "_parted", align_bytes=64)
-            nc.vector.tensor_copy(parted[:], both[:].bitcast(U16).rearrange("p (s o) -> p o s", o=PASSES))
+            halves = both[:].bitcast(U16).rearrange("p (s o) -> p o s", o=PASSES)
+            parted = [own("%s%d" % (name, o), [P, SLOTS], U16) for o in range(PASSES)]
+            for o in range(PASSES):
+                nc.vector.tensor_copy(parted[o][:], halves[:, o, :])
             return parted
 
-        kw = gather_words("kw", kw_pool, 0)
+        ks = gather_scales("ks", ks_pool)
+        cw_pool = load_word_pool("cw_pool", BAY_C, c_words)
+        cs = gather_scales("cs", cs_pool)
+        kw = gather_words("kw", kw_pool, own("kw_both", [P, SLOTS], U32))
 
-        q_codes = []
-        q_scales = []
-        for o in range(PASSES):
-            grouped = work.tile([P, NQ, PACK], BF16, name="q_grouped%d" % o, offset=(13, 7)[o] * CELL_BYTES, align_bytes=64)
-            dst = grouped[:].rearrange("p (c i) t -> p c t i", i=4)
-            src = q_raw[o][:].rearrange("p t (c i) -> p c t i", i=4)
-            if o == 0:
-                nc.scalar.copy(dst, src)
-            else:
-                nc.vector.tensor_copy(dst[:, :88], src[:, :88])
-                nc.scalar.copy(dst[:, 88:], src[:, 88:])
-            codes = held.tile([P, NQ], U32, name="q_codes%d" % o, align_bytes=64)
-            scales = held.tile([P, NQ], U8, name="q_scales%d" % o, align_bytes=64)
-            nc.vector.quantize_mx(out=codes[:].bitcast(FP8X4), scales=scales[:], in_=grouped[:].rearrange("p w j -> p (w j)"))
-            q_codes.append(codes)
-            q_scales.append(scales)
+        q_grouped = [own("q_grouped0", [P, NQ, PACK], BF16), placed("q_grouped1", [P, NQ, PACK], BF16, AT_Q1_GROUPED)]
+        q_codes = [own("q_codes%d" % o, [P, NQ], U32) for o in range(PASSES)]
+        q_scales = [own("q_scales%d" % o, [P, NQ], U8) for o in range(PASSES)]
+        copy_to = [q_grouped[o][:].rearrange("p (c i) t -> p c t i", i=4) for o in range(PASSES)]
+        copy_from = [q_raw[o][:].rearrange("p t (c i) -> p c t i", i=4) for o in range(PASSES)]
+        nc.scalar.copy(copy_to[0], copy_from[0])
+        quantise(q_codes[0][:], q_scales[0][:], q_grouped[0][:].rearrange("p q t -> p (q t)"))
+        nc.vector.tensor_copy(copy_to[1][:, :Q_SPLIT], copy_from[1][:, :Q_SPLIT])
+        nc.scalar.copy(copy_to[1][:, Q_SPLIT:], copy_from[1][:, Q_SPLIT:])
+        quantise(q_codes[1][:], q_scales[1][:], q_grouped[1][:].rearrange("p q t -> p (q t)"))
 
-        cw = gather_words("cw", cw_pool, 7)
+        cw = gather_words("cw", cw_pool, placed("cw_both", [P, SLOTS], U32, AT_Q1_GROUPED))
 
-        def load_values(e):
-            vt = ring.tile([P, TOKENS], F32, name="v_pool%d" % e, offset=(2, 3, 0, 4)[e] * SLOT_BYTES, align_bytes=64)
-            nc.sync.dma_start(vt[:], vT[e * P:(e + 1) * P, :])
-            return vt
+        v_bays = (BAY_CS, BAY_Q0, BAY_K, BAY_Q1)
+        v_pool = []
+        for e in range(E_BLOCKS):
+            v_pool.append(placed("v_pool%d" % e, [P, TOKENS], F32, v_bays[e]))
+            nc.sync.dma_start(v_pool[e][:], vT[e * P:(e + 1) * P, :])
+        og_view = og[0].rearrange("(j p) e -> p j e", p=P)
+        og_half = []
+        for h in range(2):
+            og_half.append(placed("og_half%d" % h, [P, Q_TILES, HALF], F32, BAY_C + 2 * h * CELL))
+            nc.sync.dma_start(og_half[h][:], og_view[:, :, h * HALF:(h + 1) * HALF])
 
-        v_pool = [load_values(e) for e in range(E_BLOCKS - 1)]
-        og_sb = ring.tile([P, Q_TILES, DV], F32, name="og_sb", offset=SLOT_BYTES, align_bytes=64)
-        nc.sync.dma_start(og_sb[:], og[0].rearrange("(j p) e -> p j e", p=P))
-        v_pool.append(load_values(E_BLOCKS - 1))
+
+        def score_bank(name):
+            return psum.tile([P, SLOTS], F32, name=name, tag="score", bufs=SCORE_BANKS)
 
         def score_pass(bank, j, o, words, scales):
             cols = slice(j * P, (j + 1) * P)
@@ -139,118 +166,120 @@ def tile_attend_at_proto_topk_kernel(tc, qT, k_words, k_scales, c_words, c_scale
                 out=bank[:],
                 lhsT=q_codes[o][:, cols].bitcast(FP8X4),
                 lhsT_scale=q_scales[o][:, cols],
-                rhs=words[:, o, :].bitcast(FP4X4),
+                rhs=words[o][:].bitcast(FP4X4),
                 rhs_scale=scales[o],
                 start=(o == 0),
                 stop=(o == PASSES - 1),
             )
 
-        def sigmoid_of(bank, j, name, cell):
-            sig = work.tile([P, PACK, P], F32, name=name, offset=cell * CELL_BYTES, align_bytes=64)
-            nc.scalar.activation(sig[:], bank[:].rearrange("p (s t) -> p t s", t=PACK), ACT.Sigmoid, bias=neg_th[:, j:j + 1])
+        def sigmoid_of(name, bank, j, at):
+            sig = placed(name, [P, PACK, P], F32, at + j * CELL)
+            dealt = bank[:].rearrange("p (s t) -> p t s", t=PACK)
+            nc.scalar.activation(sig[:], dealt, ACT.Sigmoid, bias=neg_th[:, j:j + 1])
             return sig
 
-        a_banks = [psum.tile([P, SLOTS], F32, name="a_bank", tag="score", bufs=4) for j in range(Q_TILES)]
+        a_banks = [score_bank("a_bank") for j in range(Q_TILES)]
         for o in range(PASSES):
             for j in range(Q_TILES):
                 score_pass(a_banks[j], j, o, kw, ks)
-        sig_a = [sigmoid_of(a_banks[j], j, "sig_a%d" % j, 9 + j) for j in range(Q_TILES)]
+        sig_a = [sigmoid_of("sig_a%d" % j, a_banks[j], j, AT_SIG_A) for j in range(Q_TILES)]
         sig_z = []
         for j in range(Q_TILES):
-            z_bank = psum.tile([P, SLOTS], F32, name="z_bank", tag="score", bufs=4)
+            z_bank = score_bank("z_bank")
             for o in range(PASSES):
                 score_pass(z_bank, j, o, cw, cs)
-            sig_z.append(sigmoid_of(z_bank, j, "sig_z%d" % j, 15 + j))
+            sig_z.append(sigmoid_of("sig_z%d" % j, z_bank, j, AT_SIG_Z))
 
-        def values_block(e):
-            if e == 3:
-                picked = ring.tile([P, SLOTS], BF16, name="v_picked3", offset=2 * SLOT_BYTES + 3 * CELL_BYTES, align_bytes=64)
-            else:
-                picked = work.tile([P, SLOTS], BF16, name="v_picked%d" % e, offset=(7, 0, 18)[e] * CELL_BYTES, align_bytes=64)
-            if e == 1:
-                rounded = work.tile([P, TOKENS], BF16, name="v_rounded", offset=8 * CELL_BYTES, align_bytes=64)
+
+        v_grouped = [own("v_grouped0", [P, HALF, PACK], BF16), placed("v_grouped1", [P, HALF, PACK], BF16, BAY_C)]
+
+        def values_block(e, picked):
+            if e == SCALAR_BLOCK:
+                rounded = placed("v_rounded", [P, TOKENS], BF16, AT_ROUNDED)
                 nc.scalar.activation(rounded[:], v_pool[e][:], ACT.Copy)
                 nc.scalar.activation(picked[:], rounded[:].indirect(offsets[:]), ACT.Copy)
             else:
                 nc.vector.tensor_copy(picked[:], v_pool[e][:].indirect(offsets[:]))
             words = picked[:].bitcast(F32)
-            bank = psum.tile([P, 2, P], F32, name="v_bank", tag="vt")
+            bank = psum.tile([P, 2, P], F32, name="v_bank", tag="turned_values")
             for u in range(2):
                 nc.tensor.transpose(bank[:, u, :], words[:, u:2 * P:2], ident[:])
-            grouped = ring.tile([P, P, PACK], BF16, name="v_grouped%d" % e, offset=(SLOT_BYTES if e == 3 else 6 * SLOT_BYTES + e * 1024), align_bytes=64)
-            nc.scalar.copy(grouped[:].bitcast(F32), bank[:].rearrange("p u e -> p e u"))
-            return grouped
+            grouped = v_grouped[e // 2][:, (e % 2) * P:(e % 2 + 1) * P, :]
+            nc.scalar.copy(grouped.bitcast(F32), bank[:].rearrange("p u e -> p e u"))
 
-        def values_quantise(e, grouped):
-            home = 5 * SLOT_BYTES + 512 if e == 0 else 4 * SLOT_BYTES + 3 * CELL_BYTES + (e - 1) * 640
-            codes = ring.tile([P, P], U32, name="v_codes%d" % e, offset=home, align_bytes=64)
-            scales = ring.tile([P, P], U8, name="v_scales%d" % e, offset=home + 512, align_bytes=64)
-            nc.vector.quantize_mx(out=codes[:].bitcast(FP8X4), scales=scales[:], in_=grouped[:].rearrange("p w j -> p (w j)"))
+        def values_quantise(h):
+            at = BAY_Q1 + (2 + h) * CELL
+            codes = placed("v_codes%d" % h, [P, HALF], U32, at)
+            scales = placed("v_scales%d" % h, [P, HALF], U8, at + 4 * HALF)
+            quantise(codes[:], scales[:], v_grouped[h][:].rearrange("p e t -> p (e t)"))
             return codes, scales
 
-        def gate_block(e):
-            gate = work.tile([P, Q_TILES, P], F32, name="gate%d" % e, offset=(8 + e) * CELL_BYTES, align_bytes=64)
-            nc.scalar.activation(gate[:], og_sb[:, :, e * P:(e + 1) * P], ACT.Sigmoid)
-            return gate
 
-        y_codes = []
-        y_scales = []
-        v_grouped = []
-        v_mx = []
-        y_half = None
-        for j in range(Q_TILES):
-            if j == 0:
-                v_grouped.append(values_block(0))
-            if j == 2:
-                v_grouped.append(values_block(1))
-            best = ring.tile([P, PACK, P], F32, name="best%d" % j, offset=2 * SLOT_BYTES + j * CELL_BYTES, align_bytes=64)
+        def turned_maximum(j):
+            best = placed("best%d" % j, [P, PACK, P], F32, BAY_CS + j * CELL)
             nc.vector.tensor_tensor(best[:], sig_a[j][:], sig_z[j][:], ALU.max)
-            bank = psum.tile([P, PACK, P], F32, name="y_bank", tag="tr")
+            bank = psum.tile([P, PACK, P], F32, name="y_bank", tag="turned_weights")
             for t in range(PACK):
                 nc.tensor.transpose(bank[:, t, :], best[:, t, :], ident[:])
-            if j == 0:
-                y_half = work.tile([P, 2, P, PACK], BF16, name="y_half0", offset=16 * CELL_BYTES, align_bytes=64)
-            if j == 2:
-                v_grouped.append(values_block(2))
-                y_half = ring.tile([P, 2, P, PACK], BF16, name="y_half1", offset=CELL_BYTES, align_bytes=64)
-            nc.vector.tensor_tensor(
-                y_half[:, j % 2],
-                bank[:].rearrange("p t q -> p q t"),
-                us_sb[:].unsqueeze(1).to_broadcast([P, P, PACK]),
-                ALU.mult,
-            )
-            if j == 1:
-                v_mx.append(values_quantise(0, v_grouped[0]))
-            if j == 3:
-                gates = [gate_block(e) for e in range(E_BLOCKS)]
-            if j % 2 == 1:
-                codes = held.tile([P, 2 * P], U32, name="y_codes%d" % j, align_bytes=64)
-                scales = held.tile([P, 2 * P], U8, name="y_scales%d" % j, align_bytes=64)
-                nc.vector.quantize_mx(out=codes[:].bitcast(FP8X4), scales=scales[:], in_=y_half[:].rearrange("p h q t -> p (h q t)"))
-                for h in range(2):
-                    y_codes.append(codes[:, h * P:(h + 1) * P])
-                    y_scales.append(scales[:, h * P:(h + 1) * P])
+            return bank
 
+        def scale_weights(y_pair, i, bank):
+            us_rows = us_sb[:].unsqueeze(1).to_broadcast([P, P, PACK])
+            nc.vector.tensor_tensor(y_pair[:, i], bank[:].rearrange("p t q -> p q t"), us_rows, ALU.mult)
+
+        def weights_quantise(pair, y_pair):
+            codes = own("y_codes%d" % pair, [P, 2 * P], U32)
+            scales = own("y_scales%d" % pair, [P, 2 * P], U8)
+            quantise(codes[:], scales[:], y_pair[:].rearrange("p i q t -> p (i q t)"))
+            return codes, scales
+
+        y_shape = [P, 2, P, PACK]
+        picked_shape = [P, SLOTS]
+
+        values_block(0, placed("v_picked0", picked_shape, BF16, AT_Q1_GROUPED))
+        bank = turned_maximum(0)
+        y_pair0 = placed("y_pair0", y_shape, BF16, AT_SIG_Z + CELL)
+        scale_weights(y_pair0, 0, bank)
+        scale_weights(y_pair0, 1, turned_maximum(1))
+        y_mx = [weights_quantise(0, y_pair0)]
+
+        values_block(1, own("v_picked1", picked_shape, BF16))
+        bank = turned_maximum(2)
+        values_block(2, placed("v_picked2", picked_shape, BF16, AT_SIG_Z + 3 * CELL))
+        y_pair1 = placed("y_pair1", y_shape, BF16, BAY_K + CELL)
+        scale_weights(y_pair1, 0, bank)
+        scale_weights(y_pair1, 1, turned_maximum(3))
+        y_mx.append(weights_quantise(1, y_pair1))
+
+
+        def gate_piece(h, pair, at):
+            gate = placed("gate%d%d" % (h, pair), [P, 2, HALF], F32, at)
+            nc.scalar.activation(gate[:], og_half[h][:, 2 * pair:2 * pair + 2, :], ACT.Sigmoid)
+            return gate
+
+        gates = [[gate_piece(0, pair, AT_ROUNDED + pair * CELL) for pair in range(2)]]
+        values_block(3, placed("v_picked3", picked_shape, BF16, BAY_CS + 3 * CELL))
+        gates.append([gate_piece(1, pair, BAY_CS + (3 - pair) * CELL) for pair in range(2)])
+        v_mx = [values_quantise(h) for h in range(2)]
+
+        result_at = ((BAY_Q1, BAY_C), (BAY_K + 2 * CELL, BAY_K + 3 * CELL))
         out_view = out[0].rearrange("(j p) e -> p j e", p=P)
-
-        def finish_block(e, v_codes, v_scales):
-            cols = slice(e * P, (e + 1) * P)
-            bank = psum.tile([P, Q_TILES, P], F32, name="o_bank", tag="score", bufs=4)
-            for j in range(Q_TILES):
-                nc.tensor.matmul_mx(
-                    out=bank[:, j, :],
-                    lhsT=y_codes[j].bitcast(FP8X4),
-                    lhsT_scale=y_scales[j],
-                    rhs=v_codes[:].bitcast(FP8X4),
-                    rhs_scale=v_scales[:],
-                    start=True,
-                    stop=True,
-                )
-            result = ring.tile([P, Q_TILES, P], F32, name="result%d" % e, offset=(4 * SLOT_BYTES + e * CELL_BYTES if e < 3 else 0), align_bytes=64)
-            nc.vector.tensor_tensor(result[:], bank[:], gates[e][:], ALU.mult)
-            nc.sync.dma_start(out_view[:, :, cols], result[:])
-
-        v_grouped.append(values_block(E_BLOCKS - 1))
-        v_mx.extend(values_quantise(e, v_grouped[e]) for e in range(1, E_BLOCKS))
-        for e in range(E_BLOCKS):
-            finish_block(e, *v_mx[e])
+        for h in range(2):
+            v_codes, v_scales = v_mx[h]
+            for pair in range(2):
+                y_codes, y_scales = y_mx[pair]
+                o_bank = psum.tile([P, 2, HALF], F32, name="o_bank", tag="score", bufs=SCORE_BANKS)
+                for i in range(2):
+                    cols = slice(i * P, (i + 1) * P)
+                    nc.tensor.matmul_mx(
+                        out=o_bank[:, i, :],
+                        lhsT=y_codes[:, cols].bitcast(FP8X4),
+                        lhsT_scale=y_scales[:, cols],
+                        rhs=v_codes[:].bitcast(FP8X4),
+                        rhs_scale=v_scales[:],
+                        start=True,
+                        stop=True,
+                    )
+                result = placed("result%d%d" % (h, pair), [P, 2, HALF], F32, result_at[h][pair])
+                nc.vector.tensor_tensor(result[:], o_bank[:], gates[h][pair][:], ALU.mult)
+                nc.sync.dma_start(out_view[:, 2 * pair:2 * pair + 2, h * HALF:(h + 1) * HALF], result[:])

from contextlib import ExitStack

import concourse.mybir as mybir
from concourse.masks import make_identity

F32 = mybir.dt.float32
BF16 = mybir.dt.bfloat16
I32 = mybir.dt.int32
U32 = mybir.dt.uint32
U16 = mybir.dt.uint16
U8 = mybir.dt.uint8
FP8X4 = mybir.dt.float8_e4m3fn_x4
FP4X4 = mybir.dt.float4_e2m1fn_x4
ACT = mybir.ActivationFunctionType
ALU = mybir.AluOpType

P = 128
PACK = 4
QUAD = 32
SLOTS = 512
TOKENS = 2048
D = 1024
NQ = 512
DV = 512
PASSES = D // (P * PACK)
Q_TILES = NQ // P
E_BLOCKS = DV // P
HALF = DV // 2
SCORE_BANKS = 4

Q_SPLIT = 88
SCALAR_BLOCK = 1

CELL = 4 * SLOTS
BAY = 4 * CELL
BAY_K = 0
BAY_Q1 = BAY
BAY_CS = 2 * BAY
BAY_Q0 = 3 * BAY
BAY_C = 4 * BAY
AT_TH = 5 * BAY
AT_Q1_GROUPED = AT_TH + CELL
AT_SIG_A = AT_Q1_GROUPED + 2 * CELL
AT_SIG_Z = AT_SIG_A + Q_TILES * CELL
AT_ROUNDED = AT_SIG_A - CELL

FLOPS = 2 * 2 * SLOTS * D * NQ + 2 * NQ * SLOTS * DV


def tile_attend_at_proto_topk_kernel(tc, qT, k_words, k_scales, c_words, c_scales, vT, th, og, us, offs, out):
    nc = tc.nc
    with ExitStack() as ctx:
        held = ctx.enter_context(tc.tile_pool(name="held", bufs=1))
        shared = ctx.enter_context(tc.tile_pool(name="shared", bufs=1))
        psum = ctx.enter_context(tc.psum_pool(name="psum", bufs=2))

        def own(name, shape, dtype):
            return held.tile(shape, dtype, name=name, align_bytes=64)

        def placed(name, shape, dtype, at):
            return shared.tile(shape, dtype, name=name, offset=at, align_bytes=64)

        def quantise(codes, scales, grouped):
            nc.vector.quantize_mx(out=codes.bitcast(FP8X4), scales=scales, in_=grouped)

        offsets = held.tile([P, SLOTS // 16], U16, name="offsets")
        nc.sync.dma_start(offsets[:], offs)


        def load_scale_pool(name, at, scales, zeroing):
            pool_tile = placed(name, [P, TOKENS], U8, at)
            zeroing.memset(pool_tile[:].bitcast(I32), 0)
            nc.sync.dma_start(pool_tile[0:P:4, :].bitcast(I32), scales.rearrange("o f t -> f o t").bitcast(I32))
            return pool_tile

        ks_pool = load_scale_pool("ks_pool", BAY_C, k_scales, nc.gpsimd)
        cs_pool = load_scale_pool("cs_pool", BAY_CS, c_scales, nc.vector)

        warm_in = placed("warm_in", [P, 8], F32, BAY_K)
        warm_out = placed("warm_out", [P, 8], F32, BAY_Q1)
        nc.vector.memset(warm_in[:], 0.0)
        nc.scalar.activation(warm_out[:], warm_in[:], ACT.Sigmoid)

        th_rows = placed("th_rows", [P, P], F32, AT_TH)
        nc.gpsimd.memset(th_rows[:], 0.0)
        nc.sync.dma_start(th_rows[0:Q_TILES, :], th[0, 0].rearrange("(j p) -> j p", p=P))
        ident = own("ident", [P, P], F32)
        make_identity(nc, ident[:])
        th_bank = psum.tile([P, P], F32, name="th_bank", tag="turned_values")
        nc.tensor.transpose(th_bank[:], th_rows[:], ident[:])
        neg_th = own("neg_th", [P, Q_TILES], F32)
        nc.scalar.activation(neg_th[:], th_bank[:, 0:Q_TILES], ACT.Copy, scale=-1.0)

        def load_word_pool(name, at, words):
            pool_tile = placed(name, [P, TOKENS], I32, at)
            nc.sync.dma_start(pool_tile[:], words[0].rearrange("p t b -> p (t b)").bitcast(I32))
            return pool_tile

        def load_queries(o, at):
            raw = placed("q_raw%d" % o, [P, PACK, NQ], F32, at)
            rows = qT[0, o * P * PACK:(o + 1) * P * PACK, :]
            nc.sync.dma_start(raw[:], rows.rearrange("(p t) q -> p t q", t=PACK))
            return raw

        q_raw = [load_queries(0, BAY_Q0)]
        kw_pool = load_word_pool("kw_pool", BAY_K, k_words)
        q_raw.append(load_queries(1, BAY_Q1))

        us_sb = placed("us_sb", [P, PACK], F32, AT_TH)
        nc.sync.dma_start(us_sb[:], us[0].rearrange("(p t) one -> p (t one)", t=PACK))


        def gather_scales(name, pool_tile):
            picked = own(name + "_picked", [P, SLOTS], U8)
            planes = own(name + "_planes", [P, PASSES * SLOTS], U8)
            nc.gpsimd.memset(planes[:].bitcast(I32), 0)
            nc.vector.tensor_copy(picked[:], pool_tile[:].indirect(offsets[:]))
            for first in range(0, P, QUAD):
                nc.sync.dma_start(planes[first:first + PACK, :].bitcast(I32), picked[first:first + QUAD:4, :].bitcast(I32))
            return [planes[:, o * SLOTS:(o + 1) * SLOTS] for o in range(PASSES)]

        def gather_words(name, pool_tile, both):
            nc.vector.tensor_copy(both[:], pool_tile[:].bitcast(U32).indirect(offsets[:]))
            halves = both[:].bitcast(U16).rearrange("p (s o) -> p o s", o=PASSES)
            parted = [own("%s%d" % (name, o), [P, SLOTS], U16) for o in range(PASSES)]
            for o in range(PASSES):
                nc.vector.tensor_copy(parted[o][:], halves[:, o, :])
            return parted

        ks = gather_scales("ks", ks_pool)
        cw_pool = load_word_pool("cw_pool", BAY_C, c_words)
        cs = gather_scales("cs", cs_pool)
        kw = gather_words("kw", kw_pool, own("kw_both", [P, SLOTS], U32))

        q_grouped = [own("q_grouped0", [P, NQ, PACK], BF16), placed("q_grouped1", [P, NQ, PACK], BF16, AT_Q1_GROUPED)]
        q_codes = [own("q_codes%d" % o, [P, NQ], U32) for o in range(PASSES)]
        q_scales = [own("q_scales%d" % o, [P, NQ], U8) for o in range(PASSES)]
        copy_to = [q_grouped[o][:].rearrange("p (c i) t -> p c t i", i=4) for o in range(PASSES)]
        copy_from = [q_raw[o][:].rearrange("p t (c i) -> p c t i", i=4) for o in range(PASSES)]
        nc.scalar.copy(copy_to[0], copy_from[0])
        quantise(q_codes[0][:], q_scales[0][:], q_grouped[0][:].rearrange("p q t -> p (q t)"))
        nc.vector.tensor_copy(copy_to[1][:, :Q_SPLIT], copy_from[1][:, :Q_SPLIT])
        nc.scalar.copy(copy_to[1][:, Q_SPLIT:], copy_from[1][:, Q_SPLIT:])
        quantise(q_codes[1][:], q_scales[1][:], q_grouped[1][:].rearrange("p q t -> p (q t)"))

        cw = gather_words("cw", cw_pool, placed("cw_both", [P, SLOTS], U32, AT_Q1_GROUPED))

        v_bays = (BAY_CS, BAY_Q0, BAY_K, BAY_Q1)
        v_pool = []
        for e in range(E_BLOCKS):
            v_pool.append(placed("v_pool%d" % e, [P, TOKENS], F32, v_bays[e]))
            nc.sync.dma_start(v_pool[e][:], vT[e * P:(e + 1) * P, :])
        og_view = og[0].rearrange("(j p) e -> p j e", p=P)
        og_half = []
        for h in range(2):
            og_half.append(placed("og_half%d" % h, [P, Q_TILES, HALF], F32, BAY_C + 2 * h * CELL))
            nc.sync.dma_start(og_half[h][:], og_view[:, :, h * HALF:(h + 1) * HALF])


        def score_bank(name):
            return psum.tile([P, SLOTS], F32, name=name, tag="score", bufs=SCORE_BANKS)

        def score_pass(bank, j, o, words, scales):
            cols = slice(j * P, (j + 1) * P)
            nc.tensor.matmul_mx(
                out=bank[:],
                lhsT=q_codes[o][:, cols].bitcast(FP8X4),
                lhsT_scale=q_scales[o][:, cols],
                rhs=words[o][:].bitcast(FP4X4),
                rhs_scale=scales[o],
                start=(o == 0),
                stop=(o == PASSES - 1),
            )

        def sigmoid_of(name, bank, j, at):
            sig = placed(name, [P, PACK, P], F32, at + j * CELL)
            dealt = bank[:].rearrange("p (s t) -> p t s", t=PACK)
            nc.scalar.activation(sig[:], dealt, ACT.Sigmoid, bias=neg_th[:, j:j + 1])
            return sig

        a_banks = [score_bank("a_bank") for j in range(Q_TILES)]
        for o in range(PASSES):
            for j in range(Q_TILES):
                score_pass(a_banks[j], j, o, kw, ks)
        sig_a = [sigmoid_of("sig_a%d" % j, a_banks[j], j, AT_SIG_A) for j in range(Q_TILES)]
        sig_z = []
        for j in range(Q_TILES):
            z_bank = score_bank("z_bank")
            for o in range(PASSES):
                score_pass(z_bank, j, o, cw, cs)
            sig_z.append(sigmoid_of("sig_z%d" % j, z_bank, j, AT_SIG_Z))


        v_grouped = [own("v_grouped0", [P, HALF, PACK], BF16), placed("v_grouped1", [P, HALF, PACK], BF16, BAY_C)]

        def values_block(e, picked):
            if e == SCALAR_BLOCK:
                rounded = placed("v_rounded", [P, TOKENS], BF16, AT_ROUNDED)
                nc.scalar.activation(rounded[:], v_pool[e][:], ACT.Copy)
                nc.scalar.activation(picked[:], rounded[:].indirect(offsets[:]), ACT.Copy)
            else:
                nc.vector.tensor_copy(picked[:], v_pool[e][:].indirect(offsets[:]))
            words = picked[:].bitcast(F32)
            bank = psum.tile([P, 2, P], F32, name="v_bank", tag="turned_values")
            for u in range(2):
                nc.tensor.transpose(bank[:, u, :], words[:, u:2 * P:2], ident[:])
            grouped = v_grouped[e // 2][:, (e % 2) * P:(e % 2 + 1) * P, :]
            nc.scalar.copy(grouped.bitcast(F32), bank[:].rearrange("p u e -> p e u"))

        def values_quantise(h):
            at = BAY_Q1 + (2 + h) * CELL
            codes = placed("v_codes%d" % h, [P, HALF], U32, at)
            scales = placed("v_scales%d" % h, [P, HALF], U8, at + 4 * HALF)
            quantise(codes[:], scales[:], v_grouped[h][:].rearrange("p e t -> p (e t)"))
            return codes, scales


        def turned_maximum(j):
            best = placed("best%d" % j, [P, PACK, P], F32, BAY_CS + j * CELL)
            nc.vector.tensor_tensor(best[:], sig_a[j][:], sig_z[j][:], ALU.max)
            bank = psum.tile([P, PACK, P], F32, name="y_bank", tag="turned_weights")
            for t in range(PACK):
                nc.tensor.transpose(bank[:, t, :], best[:, t, :], ident[:])
            return bank

        def scale_weights(y_pair, i, bank):
            us_rows = us_sb[:].unsqueeze(1).to_broadcast([P, P, PACK])
            nc.vector.tensor_tensor(y_pair[:, i], bank[:].rearrange("p t q -> p q t"), us_rows, ALU.mult)

        def weights_quantise(pair, y_pair):
            codes = own("y_codes%d" % pair, [P, 2 * P], U32)
            scales = own("y_scales%d" % pair, [P, 2 * P], U8)
            quantise(codes[:], scales[:], y_pair[:].rearrange("p i q t -> p (i q t)"))
            return codes, scales

        y_shape = [P, 2, P, PACK]
        picked_shape = [P, SLOTS]

        values_block(0, placed("v_picked0", picked_shape, BF16, AT_Q1_GROUPED))
        bank = turned_maximum(0)
        y_pair0 = placed("y_pair0", y_shape, BF16, AT_SIG_Z + CELL)
        scale_weights(y_pair0, 0, bank)
        scale_weights(y_pair0, 1, turned_maximum(1))
        y_mx = [weights_quantise(0, y_pair0)]

        values_block(1, own("v_picked1", picked_shape, BF16))
        bank = turned_maximum(2)
        values_block(2, placed("v_picked2", picked_shape, BF16, AT_SIG_Z + 3 * CELL))
        y_pair1 = placed("y_pair1", y_shape, BF16, BAY_K + CELL)
        scale_weights(y_pair1, 0, bank)
        scale_weights(y_pair1, 1, turned_maximum(3))
        y_mx.append(weights_quantise(1, y_pair1))


        def gate_piece(h, pair, at):
            gate = placed("gate%d%d" % (h, pair), [P, 2, HALF], F32, at)
            nc.scalar.activation(gate[:], og_half[h][:, 2 * pair:2 * pair + 2, :], ACT.Sigmoid)
            return gate

        gates = [[gate_piece(0, pair, AT_ROUNDED + pair * CELL) for pair in range(2)]]
        values_block(3, placed("v_picked3", picked_shape, BF16, BAY_CS + 3 * CELL))
        gates.append([gate_piece(1, pair, BAY_CS + (3 - pair) * CELL) for pair in range(2)])
        v_mx = [values_quantise(h) for h in range(2)]

        result_at = ((BAY_Q1, BAY_C), (BAY_K + 2 * CELL, BAY_K + 3 * CELL))
        out_view = out[0].rearrange("(j p) e -> p j e", p=P)
        for h in range(2):
            v_codes, v_scales = v_mx[h]
            for pair in range(2):
                y_codes, y_scales = y_mx[pair]
                o_bank = psum.tile([P, 2, HALF], F32, name="o_bank", tag="score", bufs=SCORE_BANKS)
                for i in range(2):
                    cols = slice(i * P, (i + 1) * P)
                    nc.tensor.matmul_mx(
                        out=o_bank[:, i, :],
                        lhsT=y_codes[:, cols].bitcast(FP8X4),
                        lhsT_scale=y_scales[:, cols],
                        rhs=v_codes[:].bitcast(FP8X4),
                        rhs_scale=v_scales[:],
                        start=True,
                        stop=True,
                    )
                result = placed("result%d%d" % (h, pair), [P, 2, HALF], F32, result_at[h][pair])
                nc.vector.tensor_tensor(result[:], o_bank[:], gates[h][pair][:], ALU.mult)
                nc.sync.dma_start(out_view[:, 2 * pair:2 * pair + 2, h * HALF:(h + 1) * HALF], result[:])
